import numpy as np
import ml_dtypes


def mxq(x, axis, fmt="e4m3"):
    dtype, down = {"e4m3": (ml_dtypes.float8_e4m3fn, 7), "e5m2": (ml_dtypes.float8_e5m2, 14)}[fmt]
    v = np.moveaxis(np.asarray(x, np.float32).astype(ml_dtypes.bfloat16).astype(np.float64), axis, -1)
    blocks = v.reshape(v.shape[:-1] + (-1, 32))
    amax = np.abs(blocks).max(-1, keepdims=True)
    byte = np.maximum(np.where(amax > 0, np.frexp(amax)[1] - 1 + 127, 0) - down, 1)
    scale = np.exp2(byte - 127.0)
    codes = (blocks / scale).astype(np.float32).astype(dtype).astype(np.float64)
    return np.moveaxis((codes * scale).reshape(v.shape), -1, axis)


WIDE = False


def mx_kscale(k):
    if not WIDE:
        return np.ones(k)
    levels = np.array([10, -10, 5, -5, 0])
    if k % 512:
        return np.exp2(np.random.permutation(np.resize(levels, k // 32))).repeat(32)
    a = np.empty((k // 512, 16))
    for p in range(k // 512):
        a[p, :8] = np.random.permutation(np.resize(levels, 8))
        for g in range(8):
            far = levels[np.abs(levels - a[p, g]) >= 10]
            a[p, g + 8] = far[np.random.randint(len(far))]
    return np.exp2(a.ravel()).repeat(32)


def f64(x):
    return np.asarray(x).astype(np.float64)


def striped(idx):
    return np.tile(idx.reshape(-1, 16).T, (8, 1)).astype(np.uint16)


def unstriped(offs):
    return offs[:16].T.reshape(-1).astype(np.int64)


def striped8(idx):
    return np.concatenate([x.reshape(-1, 16).T for x in idx]).astype(np.uint16)


def runs(offs, k):
    lists = np.stack([offs[16 * r : 16 * r + 16].T.reshape(-1) for r in range(8)]).astype(np.int64)
    return lists[np.arange(k) % 512 // 64]


def pack_weight(w):
    k, n = w.shape
    w = f64(np.asarray(w, np.float32).astype(ml_dtypes.bfloat16)).reshape(k // 32, 32, n)
    amax = np.abs(w).max(1)
    byte = np.clip(np.where(amax > 0, np.frexp(amax)[1] - 1 + 127 - 7, 1), 1, 254)
    scaled = (w * np.exp2(127.0 - byte)[:, None, :]).reshape(k, n).astype(np.float32)
    words = np.ascontiguousarray(scaled.reshape(k // 512, 128, 4, n).transpose(0, 1, 3, 2)).astype(ml_dtypes.float8_e4m3fn).view(np.uint8)
    return words, np.ascontiguousarray(byte.astype(np.uint8).reshape(k // 512, 16, n))


def unpack_weight(words, scales):
    g, p, n, _ = words.shape
    vals = np.ascontiguousarray(words).view(ml_dtypes.float8_e4m3fn).astype(np.float64) * np.repeat(np.exp2(scales.astype(np.float64) - 127.0), 8, axis=1)[..., None]
    return vals.transpose(0, 1, 3, 2).reshape(g * 512, n)


K, T, S, V, H, J = 512, 2048, 512, 512, 512, 512


def setup_inputs():
    n = np.random.standard_normal
    s = mx_kscale(K)[:, None]
    u = mx_kscale(S)
    packed_xT = pack_weight(n((K, T)) * s)
    return {
        "x_words": packed_xT[0],
        "x_scales": packed_xT[1],
        "w1": (n((K, H)) / np.sqrt(K) / s).astype(np.float32),
        "w2": (n((K, H)) / np.sqrt(K) / s).astype(np.float32),
        "ga": (np.random.uniform(0.5, 1.5, (H, 1)) * u[:, None]).astype(np.float32),
        "gb": (np.random.uniform(0.5, 1.5, (H, 1)) / u[:, None]).astype(np.float32),
        "tab": n((S, J)).astype(np.float32),
        "offs": striped(np.random.permutation(T)[:S]),
        "two": striped(np.random.permutation(T)[:V]),
        "n1": striped8(np.stack([np.random.permutation(S) for _ in range(8)])),
        "n2": striped8(np.stack([np.random.permutation(S) for _ in range(8)])),
        "n3": striped8(np.stack([np.random.permutation(V) for _ in range(8)])),
        "n4": striped8(np.stack([np.random.permutation(V) for _ in range(8)])),
        "n5": striped8(np.random.randint(0, J, (8, V))),
        "n6": striped8(np.random.randint(0, J, (8, V))),
        "n7": striped8(np.stack([np.random.permutation(V) for _ in range(8)])),
    }


def reference(x_words, x_scales, w1, w2, ga, gb, tab, offs, two, n1, n2, n3, n4, n5, n6, n7):
    xq = unpack_weight(x_words, x_scales)[:, unstriped(offs)]
    a = mxq(f64(w1), 0, "e4m3").T @ xq
    st = a + 0.5 * (a[np.arange(H)[:, None], runs(n1, H)])
    z = f64(ga) * (st - (st[np.arange(H)[:, None], runs(n2, H)]))
    x_two = unpack_weight(x_words, x_scales)[:, unstriped(two)]
    b = mxq(f64(w2), 0, "e4m3").T @ x_two
    z2 = f64(gb) * (np.maximum(b[np.arange(H)[:, None], runs(n3, H)], b[np.arange(H)[:, None], runs(n4, H)]) - (0.75 * b))
    s = 0.0625 * ((mxq(z, 0, "e4m3").T @ mxq(z2, 0, "e4m3")))
    return (s[np.arange(S)[:, None], runs(n7, S)]) * (f64(tab)[np.arange(S)[:, None], runs(n5, S)]) + f64(tab)[np.arange(S)[:, None], runs(n6, S)]

@@ -1,0 +1,189 @@
+from contextlib import ExitStack
+
+import concourse.mybir as mybir
+
+F32 = mybir.dt.float32
+BF16 = mybir.dt.bfloat16
+I32 = mybir.dt.int32
+U32 = mybir.dt.uint32
+U16 = mybir.dt.uint16
+U8 = mybir.dt.uint8
+FP8X4 = mybir.dt.float8_e4m3fn_x4
+ALU = mybir.AluOpType
+COPY = mybir.ActivationFunctionType.Copy
+
+P = 128
+PACK = 4
+N = 512
+T = 2048
+FLOPS = 3 * 2 * 512 * 512 * 512
+
+
+def tile_picked_kqhopoverkinda_none_p_kernel(
+    tc, x_words, x_scales, w1, w2, ga, gb, tab, offs, two, n1, n2, n3, n4, n5, n6, n7, out
+):
+    nc = tc.nc
+    with ExitStack() as ctx:
+        sb = ctx.enter_context(tc.tile_pool(name="sb", bufs=1))
+        ps = ctx.enter_context(tc.psum_pool(name="ps", bufs=1))
+
+        def tile(name, shape, dtype):
+            return sb.tile(shape, dtype, name=name, align_bytes=64)
+
+        def load_list(name, src):
+            lst = tile(name, [P, N // 16], U16)
+            nc.sync.dma_start(lst[:], src)
+            return lst
+
+        planes = range(PACK)
+        tab_rows = tab.rearrange("(p u) j -> p u j", u=PACK)
+        out_rows = out.rearrange("(p u) v -> p u v", u=PACK)
+
+        xw = tile("xw", [P, T], U32)
+        xs = tile("xs", [P, T], U8)
+        tab_win = [tile("tab_win%d" % u, [P, 2 * N], F32) for u in planes]
+        bs_win = [tile("bs_win%d" % t, [P, 2 * N], F32) for t in planes]
+        half_win = [tile("half_win%d" % t, [P, 2 * N], F32) for t in planes]
+        st_win = [tile("st_win%d" % t, [P, 2 * N], F32) for t in planes]
+
+        nc.vector.memset(xs[:].bitcast(I32), 0)
+        for win in tab_win[:1] + bs_win + tab_win[1:]:
+            nc.vector.memset(win[:, N:], 0.0)
+
+        l5 = load_list("l5", n5)
+        nc.sync.dma_start(tab_win[0][:, :N], tab_rows[:, 0, :])
+        nc.sync.dma_start(xw[:].bitcast(I32), x_words[0].rearrange("p n t -> p (n t)").bitcast(I32))
+        l_two = load_list("l_two", two)
+        for q in range(4):
+            nc.scalar.dma_start(xs[32 * q : 32 * q + 4, :].bitcast(I32), x_scales[0, 4 * q : 4 * q + 4, :].bitcast(I32))
+        w2_raw = tile("w2_raw", [P, PACK, N], F32)
+        nc.sync.dma_start(w2_raw[:], w2.rearrange("(p j) c -> p j c", j=PACK))
+        gb4 = tile("gb4", [P, PACK], F32)
+        ga4 = tile("ga4", [P, PACK], F32)
+        nc.gpsimd.dma_start(gb4[:], gb.rearrange("(p t) o -> p (t o)", t=PACK))
+        nc.gpsimd.dma_start(ga4[:], ga.rearrange("(p t) o -> p (t o)", t=PACK))
+        l_offs = load_list("l_offs", offs)
+        l3 = load_list("l3", n3)
+        l4 = load_list("l4", n4)
+        w1_raw = tile("w1_raw", [P, PACK, N], F32)
+        nc.sync.dma_start(w1_raw[:], w1.rearrange("(p j) c -> p j c", j=PACK))
+        l1 = load_list("l1", n1)
+        l2 = load_list("l2", n2)
+        l7 = load_list("l7", n7)
+        l6 = load_list("l6", n6)
+        for u in range(1, PACK):
+            nc.sync.dma_start(tab_win[u][:, :N], tab_rows[:, u, :])
+
+        t5_first = tile("t5_first", [P, N], F32)
+        nc.vector.tensor_copy(t5_first[:], tab_win[0][:].indirect(l5[:]))
+
+        sign2 = tile("sign2", [P, PACK], F32)
+        sign = tile("sign", [P, PACK], F32)
+        b_scale = tile("b_scale", [P, PACK], F32)
+        c_scale = tile("c_scale", [P, PACK], F32)
+        a_scale = tile("a_scale", [P, PACK], F32)
+        h_scale = tile("h_scale", [P, PACK], F32)
+        nc.vector.tensor_scalar(sign2[:], gb4[:], 0.0, 2.0, ALU.is_ge, ALU.mult)
+        nc.vector.tensor_scalar(sign[:], sign2[:], -1.0, None, ALU.add)
+        nc.vector.tensor_tensor(b_scale[:], gb4[:], sign[:], ALU.mult)
+        nc.vector.tensor_tensor(a_scale[:], ga4[:], sign[:], ALU.mult)
+        nc.vector.tensor_scalar(c_scale[:], b_scale[:], 0.75, None, ALU.mult)
+        nc.vector.tensor_scalar(h_scale[:], a_scale[:], -0.5, None, ALU.mult)
+
+        def pick_tokens(name, lst):
+            words = tile(name + "_words", [P, N], U32)
+            scales = tile(name + "_scales", [P, N], U8)
+            nc.vector.tensor_copy(words[:], xw[:].indirect(lst[:]))
+            nc.vector.tensor_copy(scales[:], xs[:].indirect(lst[:]))
+            return words, scales
+
+        def deal(name, raw, h):
+            dealt = tile("%s_dealt%d" % (name, h), [P, 2 * P * PACK], BF16)
+            nc.scalar.copy(
+                dealt[:].rearrange("p (e m j) -> p m j e", e=2, j=PACK),
+                raw[:].rearrange("p j (m t) -> p m j t", t=PACK)[:, :, :, 2 * h : 2 * h + 2],
+            )
+            return dealt
+
+        def quantise(name, src, width):
+            codes = tile(name + "_codes", [P, width], U32)
+            scales = tile(name + "_scales", [P, width], U8)
+            nc.vector.quantize_mx(out=codes[:].bitcast(FP8X4), scales=scales[:], in_=src[:])
+            return codes, scales
+
+        def product(bank, stationary, e, moving):
+            acc = ps.tile([P, N], F32, name=bank)
+            cols = slice(e * P, (e + 1) * P)
+            nc.tensor.matmul_mx(
+                out=acc[:],
+                lhsT=stationary[0][:, cols].bitcast(FP8X4),
+                lhsT_scale=stationary[1][:, cols],
+                rhs=moving[0][:].bitcast(FP8X4),
+                rhs_scale=moving[1][:],
+                start=True,
+                stop=True,
+            )
+            return acc
+
+        x_two = pick_tokens("x_two", l_two)
+        x_offs = pick_tokens("x_offs", l_offs)
+
+        u4 = tile("u4", [P, PACK, N], F32)
+        v4 = tile("v4", [P, PACK, N], F32)
+        w2_q = [quantise("w2_%d" % h, deal("w2", w2_raw, h), 2 * P) for h in range(2)]
+        for t in planes:
+            acc = product("bank_b%d" % t, w2_q[t // 2], t % 2, x_two)
+            nc.scalar.activation(bs_win[t][:, :N], acc[:], COPY, scale=b_scale[:, t : t + 1])
+            nc.scalar.activation(half_win[t][:, N:], acc[:], COPY, scale=c_scale[:, t : t + 1])
+        for t in planes:
+            nc.vector.tensor_tensor(u4[:, t, :], bs_win[t][:].indirect(l3[:]), half_win[t][:, N:], ALU.subtract)
+            nc.vector.tensor_tensor(v4[:, t, :], bs_win[t][:].indirect(l4[:]), half_win[t][:, N:], ALU.subtract)
+
+        w1_q = [quantise("w1_%d" % h, deal("w1", w1_raw, h), 2 * P) for h in range(2)]
+        for t in planes:
+            acc = product("bank_a%d" % t, w1_q[t // 2], t % 2, x_offs)
+            nc.scalar.activation(half_win[t][:, :N], acc[:], COPY, scale=h_scale[:, t : t + 1])
+            nc.scalar.activation(st_win[t][:, N:], acc[:], COPY, scale=a_scale[:, t : t + 1])
+        st4 = tile("st4", [P, PACK, N], F32)
+        for t in planes:
+            nc.vector.tensor_tensor(st_win[t][:, :N], half_win[t][:].indirect(l1[:]), st_win[t][:, N:], ALU.subtract)
+            nc.scalar.activation(st4[:, t, :], st_win[t][:, :N], COPY, scale=-1.0)
+
+        u_bf = tile("u_bf", [P, N * PACK], BF16)
+        v_bf = tile("v_bf", [P, N * PACK], BF16)
+        for src, dst in ((u4, u_bf), (v4, v_bf)):
+            for h in range(2):
+                nc.scalar.copy(
+                    dst[:, h * 2 * N : (h + 1) * 2 * N].rearrange("p (c i t) -> p c t i", i=4, t=PACK),
+                    src[:, :, h * N // 2 : (h + 1) * N // 2].rearrange("p t (c i) -> p c t i", i=4),
+                )
+
+        z4 = tile("z4", [P, PACK, N], F32)
+        for t in planes:
+            nc.vector.tensor_tensor(z4[:, t, :], st_win[t][:].indirect(l2[:]), st4[:, t, :], ALU.add)
+
+        z2_bf = tile("z2_bf", [P, N * PACK], BF16)
+        nc.vector.tensor_tensor(z2_bf[:], u_bf[:], v_bf[:], ALU.max)
+        z2_q = quantise("z2", z2_bf, N)
+
+        z_dealt = [deal("z", z4, h) for h in range(2)]
+        t5_late = tile("st4", [P, PACK, N], F32)
+        t5 = [t5_first[:]] + [t5_late[:, u, :] for u in range(1, PACK)]
+        nc.vector.tensor_copy(t5[1], tab_win[1][:].indirect(l5[:]))
+        z_q = [quantise("z_0", z_dealt[0], 2 * P)]
+        nc.vector.tensor_copy(t5[2], tab_win[2][:].indirect(l5[:]))
+        z_q.append(quantise("z_1", z_dealt[1], 2 * P))
+        nc.vector.tensor_copy(t5[3], tab_win[3][:].indirect(l5[:]))
+
+        for u in planes:
+            acc = product("bank_b%d" % u, z_q[u // 2], u % 2, z2_q)
+            nc.scalar.activation(bs_win[u][:, :N], acc[:], COPY, scale=0.0625)
+        prod = [tile("prod%d" % u, [P, N], F32) for u in planes]
+        res = [tile("res%d" % u, [P, N], F32) for u in planes]
+        for step in range(PACK + 1):
+            if step < PACK:
+                nc.vector.tensor_tensor(prod[step][:], bs_win[step][:].indirect(l7[:]), t5[step], ALU.mult)
+            if step > 0:
+                u = step - 1
+                nc.vector.tensor_tensor(res[u][:], tab_win[u][:].indirect(l6[:]), prod[u][:], ALU.add)
+                nc.sync.dma_start(out_rows[:, u, :], res[u][:])

@@ -46,36 +46,38 @@ def tile_picked_kqhopoverkinda_none_p_kernel(
         half_win = [tile("half_win%d" % t, [P, 2 * N], F32) for t in planes]
         st_win = [tile("st_win%d" % t, [P, 2 * N], F32) for t in planes]
 
-        nc.vector.memset(xs[:].bitcast(I32), 0)
-        for win in tab_win[:1] + bs_win + tab_win[1:]:
+        nc.gpsimd.memset(xs[:].bitcast(I32), 0)
+        for win in tab_win[:2] + bs_win[:2]:
             nc.vector.memset(win[:, N:], 0.0)
+        for win in tab_win[2:3] + bs_win[2:] + tab_win[3:]:
+            nc.gpsimd.memset(win[:, N:], 0.0)
 
-        l5 = load_list("l5", n5)
         nc.sync.dma_start(tab_win[0][:, :N], tab_rows[:, 0, :])
-        nc.sync.dma_start(xw[:].bitcast(I32), x_words[0].rearrange("p n t -> p (n t)").bitcast(I32))
+        l5 = load_list("l5", n5)
+        nc.sync.dma_start(tab_win[1][:, :N], tab_rows[:, 1, :])
         l_two = load_list("l_two", two)
         for q in range(4):
             nc.scalar.dma_start(xs[32 * q : 32 * q + 4, :].bitcast(I32), x_scales[0, 4 * q : 4 * q + 4, :].bitcast(I32))
-        w2_raw = tile("w2_raw", [P, PACK, N], F32)
+        w2_raw = tile("w_raw", [P, PACK, N], F32)
         nc.sync.dma_start(w2_raw[:], w2.rearrange("(p j) c -> p j c", j=PACK))
         gb4 = tile("gb4", [P, PACK], F32)
         ga4 = tile("ga4", [P, PACK], F32)
-        nc.gpsimd.dma_start(gb4[:], gb.rearrange("(p t) o -> p (t o)", t=PACK))
-        nc.gpsimd.dma_start(ga4[:], ga.rearrange("(p t) o -> p (t o)", t=PACK))
+        nc.sync.dma_start(gb4[:], gb.rearrange("(p t) o -> p (t o)", t=PACK))
         l_offs = load_list("l_offs", offs)
+        nc.sync.dma_start(xw[:].bitcast(I32), x_words[0].rearrange("p n t -> p (n t)").bitcast(I32))
+        nc.sync.dma_start(tab_win[2][:, :N], tab_rows[:, 2, :])
         l3 = load_list("l3", n3)
         l4 = load_list("l4", n4)
-        w1_raw = tile("w1_raw", [P, PACK, N], F32)
-        nc.sync.dma_start(w1_raw[:], w1.rearrange("(p j) c -> p j c", j=PACK))
+        nc.sync.dma_start(ga4[:], ga.rearrange("(p t) o -> p (t o)", t=PACK))
         l1 = load_list("l1", n1)
         l2 = load_list("l2", n2)
         l7 = load_list("l7", n7)
         l6 = load_list("l6", n6)
-        for u in range(1, PACK):
-            nc.sync.dma_start(tab_win[u][:, :N], tab_rows[:, u, :])
+        nc.sync.dma_start(tab_win[3][:, :N], tab_rows[:, 3, :])
 
-        t5_first = tile("t5_first", [P, N], F32)
-        nc.vector.tensor_copy(t5_first[:], tab_win[0][:].indirect(l5[:]))
+        t5 = [tile("t5_%d" % u, [P, N], F32) for u in range(PACK - 1)]
+        for u in range(2):
+            nc.vector.tensor_copy(t5[u][:], tab_win[u][:].indirect(l5[:]))
 
         sign2 = tile("sign2", [P, PACK], F32)
         sign = tile("sign", [P, PACK], F32)
@@ -83,24 +85,21 @@ def tile_picked_kqhopoverkinda_none_p_kernel(
         c_scale = tile("c_scale", [P, PACK], F32)
         a_scale = tile("a_scale", [P, PACK], F32)
         h_scale = tile("h_scale", [P, PACK], F32)
-        nc.vector.tensor_scalar(sign2[:], gb4[:], 0.0, 2.0, ALU.is_ge, ALU.mult)
-        nc.vector.tensor_scalar(sign[:], sign2[:], -1.0, None, ALU.add)
-        nc.vector.tensor_tensor(b_scale[:], gb4[:], sign[:], ALU.mult)
-        nc.vector.tensor_tensor(a_scale[:], ga4[:], sign[:], ALU.mult)
-        nc.vector.tensor_scalar(c_scale[:], b_scale[:], 0.75, None, ALU.mult)
-        nc.vector.tensor_scalar(h_scale[:], a_scale[:], -0.5, None, ALU.mult)
+        nc.gpsimd.tensor_scalar(sign2[:], gb4[:], 0.0, 2.0, ALU.is_ge, ALU.mult)
+        nc.gpsimd.tensor_scalar(sign[:], sign2[:], -1.0, None, ALU.add)
+        nc.gpsimd.tensor_tensor(b_scale[:], gb4[:], sign[:], ALU.mult)
+        nc.gpsimd.tensor_tensor(a_scale[:], ga4[:], sign[:], ALU.mult)
+        nc.gpsimd.tensor_scalar(c_scale[:], b_scale[:], 0.75, None, ALU.mult)
+        nc.gpsimd.tensor_scalar(h_scale[:], a_scale[:], -0.5, None, ALU.mult)
 
-        def pick_tokens(name, lst):
-            words = tile(name + "_words", [P, N], U32)
-            scales = tile(name + "_scales", [P, N], U8)
-            nc.vector.tensor_copy(words[:], xw[:].indirect(lst[:]))
-            nc.vector.tensor_copy(scales[:], xs[:].indirect(lst[:]))
-            return words, scales
+        def pick(name, table, lst, dtype):
+            picked = tile(name, [P, N], dtype)
+            nc.vector.tensor_copy(picked[:], table[:].indirect(lst[:]))
+            return picked
 
-        def deal(name, raw, h):
-            dealt = tile("%s_dealt%d" % (name, h), [P, 2 * P * PACK], BF16)
+        def deal(dealt, raw, h):
             nc.scalar.copy(
-                dealt[:].rearrange("p (e m j) -> p m j e", e=2, j=PACK),
+                dealt.rearrange("p (e m j) -> p m j e", e=2, j=PACK),
                 raw[:].rearrange("p j (m t) -> p m j t", t=PACK)[:, :, :, 2 * h : 2 * h + 2],
             )
             return dealt
@@ -108,7 +107,7 @@ def tile_picked_kqhopoverkinda_none_p_kernel(
         def quantise(name, src, width):
             codes = tile(name + "_codes", [P, width], U32)
             scales = tile(name + "_scales", [P, width], U8)
-            nc.vector.quantize_mx(out=codes[:].bitcast(FP8X4), scales=scales[:], in_=src[:])
+            nc.vector.quantize_mx(out=codes[:].bitcast(FP8X4), scales=scales[:], in_=src)
             return codes, scales
 
         def product(bank, stationary, e, moving):
@@ -125,55 +124,57 @@ def tile_picked_kqhopoverkinda_none_p_kernel(
             )
             return acc
 
-        x_two = pick_tokens("x_two", l_two)
-        x_offs = pick_tokens("x_offs", l_offs)
+        two_scales = pick("two_scales", xs, l_two, U8)
+        offs_scales = pick("offs_scales", xs, l_offs, U8)
+        x_two = (pick("two_words", xw, l_two, U32), two_scales)
+        x_offs = (pick("offs_words", xw, l_offs, U32), offs_scales)
 
+        nc.vector.tensor_copy(t5[2][:], tab_win[2][:].indirect(l5[:]))
         u4 = tile("u4", [P, PACK, N], F32)
-        v4 = tile("v4", [P, PACK, N], F32)
-        w2_q = [quantise("w2_%d" % h, deal("w2", w2_raw, h), 2 * P) for h in range(2)]
+        w2_bf = tile("w2_bf", [P, 2, 2 * N], BF16)
+        w2_q = [quantise("w2_%d" % h, deal(w2_bf[:, h, :], w2_raw, h), 2 * P) for h in range(2)]
+        w1_raw = tile("w_raw", [P, PACK, N], F32)
+        nc.sync.dma_start(w1_raw[:], w1.rearrange("(p j) c -> p j c", j=PACK))
         for t in planes:
             acc = product("bank_b%d" % t, w2_q[t // 2], t % 2, x_two)
             nc.scalar.activation(bs_win[t][:, :N], acc[:], COPY, scale=b_scale[:, t : t + 1])
             nc.scalar.activation(half_win[t][:, N:], acc[:], COPY, scale=c_scale[:, t : t + 1])
         for t in planes:
             nc.vector.tensor_tensor(u4[:, t, :], bs_win[t][:].indirect(l3[:]), half_win[t][:, N:], ALU.subtract)
-            nc.vector.tensor_tensor(v4[:, t, :], bs_win[t][:].indirect(l4[:]), half_win[t][:, N:], ALU.subtract)
 
-        w1_q = [quantise("w1_%d" % h, deal("w1", w1_raw, h), 2 * P) for h in range(2)]
+        w1_bf = tile("v4", [P, 2, 2 * N], BF16)
+        w1_q = [quantise("w1_%d" % h, deal(w1_bf[:, h, :], w1_raw, h), 2 * P) for h in range(2)]
+        v4 = tile("v4", [P, PACK, N], F32)
+        for t in planes:
+            nc.vector.tensor_tensor(v4[:, t, :], bs_win[t][:].indirect(l4[:]), half_win[t][:, N:], ALU.subtract)
         for t in planes:
             acc = product("bank_a%d" % t, w1_q[t // 2], t % 2, x_offs)
             nc.scalar.activation(half_win[t][:, :N], acc[:], COPY, scale=h_scale[:, t : t + 1])
             nc.scalar.activation(st_win[t][:, N:], acc[:], COPY, scale=a_scale[:, t : t + 1])
         st4 = tile("st4", [P, PACK, N], F32)
+        u_bf = tile("offs_words", [P, N * PACK], BF16)
+        v_bf = tile("offs_scales", [P, N * PACK], BF16)
         for t in planes:
+            src, dst, h = (u4, v4)[t // 2], (u_bf, v_bf)[t // 2], t % 2
+            nc.scalar.copy(
+                dst[:, h * 2 * N : (h + 1) * 2 * N].rearrange("p (c i t) -> p c t i", i=4, t=PACK),
+                src[:, :, h * N // 2 : (h + 1) * N // 2].rearrange("p t (c i) -> p c t i", i=4),
+            )
             nc.vector.tensor_tensor(st_win[t][:, :N], half_win[t][:].indirect(l1[:]), st_win[t][:, N:], ALU.subtract)
             nc.scalar.activation(st4[:, t, :], st_win[t][:, :N], COPY, scale=-1.0)
-
-        u_bf = tile("u_bf", [P, N * PACK], BF16)
-        v_bf = tile("v_bf", [P, N * PACK], BF16)
-        for src, dst in ((u4, u_bf), (v4, v_bf)):
-            for h in range(2):
-                nc.scalar.copy(
-                    dst[:, h * 2 * N : (h + 1) * 2 * N].rearrange("p (c i t) -> p c t i", i=4, t=PACK),
-                    src[:, :, h * N // 2 : (h + 1) * N // 2].rearrange("p t (c i) -> p c t i", i=4),
-                )
 
         z4 = tile("z4", [P, PACK, N], F32)
         for t in planes:
             nc.vector.tensor_tensor(z4[:, t, :], st_win[t][:].indirect(l2[:]), st4[:, t, :], ALU.add)
 
-        z2_bf = tile("z2_bf", [P, N * PACK], BF16)
+        z_dealt = [deal(tile("z_dealt%d" % h, [P, 2 * N], BF16)[:], z4, h) for h in range(2)]
+        z2_bf = tile("st4", [P, N * PACK], BF16)
         nc.vector.tensor_tensor(z2_bf[:], u_bf[:], v_bf[:], ALU.max)
-        z2_q = quantise("z2", z2_bf, N)
-
-        z_dealt = [deal("z", z4, h) for h in range(2)]
-        t5_late = tile("st4", [P, PACK, N], F32)
-        t5 = [t5_first[:]] + [t5_late[:, u, :] for u in range(1, PACK)]
-        nc.vector.tensor_copy(t5[1], tab_win[1][:].indirect(l5[:]))
+        z2_q = quantise("z2", z2_bf[:], N)
         z_q = [quantise("z_0", z_dealt[0], 2 * P)]
-        nc.vector.tensor_copy(t5[2], tab_win[2][:].indirect(l5[:]))
+        t5.append(tile("z_dealt0", [P, N], F32))
+        nc.vector.tensor_copy(t5[3][:], tab_win[3][:].indirect(l5[:]))
         z_q.append(quantise("z_1", z_dealt[1], 2 * P))
-        nc.vector.tensor_copy(t5[3], tab_win[3][:].indirect(l5[:]))
 
         for u in planes:
             acc = product("bank_b%d" % u, z_q[u // 2], u % 2, z2_q)
@@ -182,7 +183,7 @@ def tile_picked_kqhopoverkinda_none_p_kernel(
         res = [tile("res%d" % u, [P, N], F32) for u in planes]
         for step in range(PACK + 1):
             if step < PACK:
-                nc.vector.tensor_tensor(prod[step][:], bs_win[step][:].indirect(l7[:]), t5[step], ALU.mult)
+                nc.vector.tensor_tensor(prod[step][:], bs_win[step][:].indirect(l7[:]), t5[step][:], ALU.mult)
             if step > 0:
                 u = step - 1
                 nc.vector.tensor_tensor(res[u][:], tab_win[u][:].indirect(l6[:]), prod[u][:], ALU.add)

@@ -10,6 +10,7 @@ U16 = mybir.dt.uint16
 U8 = mybir.dt.uint8
 FP8X4 = mybir.dt.float8_e4m3fn_x4
 ALU = mybir.AluOpType
+ABS = mybir.ActivationFunctionType.Abs
 COPY = mybir.ActivationFunctionType.Copy
 
 P = 128
@@ -63,12 +64,12 @@ def tile_picked_kqhopoverkinda_none_p_kernel(
         gb4 = tile("gb4", [P, PACK], F32)
         ga4 = tile("ga4", [P, PACK], F32)
         nc.sync.dma_start(gb4[:], gb.rearrange("(p t) o -> p (t o)", t=PACK))
+        nc.sync.dma_start(ga4[:], ga.rearrange("(p t) o -> p (t o)", t=PACK))
         l_offs = load_list("l_offs", offs)
         nc.sync.dma_start(xw[:].bitcast(I32), x_words[0].rearrange("p n t -> p (n t)").bitcast(I32))
         nc.sync.dma_start(tab_win[2][:, :N], tab_rows[:, 2, :])
         l3 = load_list("l3", n3)
         l4 = load_list("l4", n4)
-        nc.sync.dma_start(ga4[:], ga.rearrange("(p t) o -> p (t o)", t=PACK))
         l1 = load_list("l1", n1)
         l2 = load_list("l2", n2)
         l7 = load_list("l7", n7)
@@ -87,14 +88,16 @@ def tile_picked_kqhopoverkinda_none_p_kernel(
         h_scale = tile("h_scale", [P, PACK], F32)
         nc.gpsimd.tensor_scalar(sign2[:], gb4[:], 0.0, 2.0, ALU.is_ge, ALU.mult)
         nc.gpsimd.tensor_scalar(sign[:], sign2[:], -1.0, None, ALU.add)
-        nc.gpsimd.tensor_tensor(b_scale[:], gb4[:], sign[:], ALU.mult)
+        nc.scalar.activation(b_scale[:], gb4[:], ABS)
         nc.gpsimd.tensor_tensor(a_scale[:], ga4[:], sign[:], ALU.mult)
-        nc.gpsimd.tensor_scalar(c_scale[:], b_scale[:], 0.75, None, ALU.mult)
+        nc.scalar.activation(c_scale[:], gb4[:], ABS, scale=0.75)
         nc.gpsimd.tensor_scalar(h_scale[:], a_scale[:], -0.5, None, ALU.mult)
 
-        def pick(name, table, lst, dtype):
+        def pick(name, table, lst, dtype, pieces=1):
             picked = tile(name, [P, N], dtype)
-            nc.vector.tensor_copy(picked[:], table[:].indirect(lst[:]))
+            for i in range(pieces):
+                cols = slice(i * N // pieces, (i + 1) * N // pieces)
+                nc.vector.tensor_copy(picked[:, cols], table[:].indirect(lst[:, cols.start // 16 : cols.stop // 16]))
             return picked
 
         def deal(dealt, raw, h):
@@ -110,15 +113,15 @@ def tile_picked_kqhopoverkinda_none_p_kernel(
             nc.vector.quantize_mx(out=codes[:].bitcast(FP8X4), scales=scales[:], in_=src)
             return codes, scales
 
-        def product(bank, stationary, e, moving):
-            acc = ps.tile([P, N], F32, name=bank)
+        def product(bank, stationary, e, moving, part=slice(0, N)):
+            acc = ps.tile([P, part.stop - part.start], F32, name=bank)
             cols = slice(e * P, (e + 1) * P)
             nc.tensor.matmul_mx(
                 out=acc[:],
                 lhsT=stationary[0][:, cols].bitcast(FP8X4),
                 lhsT_scale=stationary[1][:, cols],
-                rhs=moving[0][:].bitcast(FP8X4),
-                rhs_scale=moving[1][:],
+                rhs=moving[0][:, part].bitcast(FP8X4),
+                rhs_scale=moving[1][:, part],
                 start=True,
                 stop=True,
             )
@@ -126,7 +129,7 @@ def tile_picked_kqhopoverkinda_none_p_kernel(
 
         two_scales = pick("two_scales", xs, l_two, U8)
         offs_scales = pick("offs_scales", xs, l_offs, U8)
-        x_two = (pick("two_words", xw, l_two, U32), two_scales)
+        x_two = (pick("two_words", xw, l_two, U32, 2), two_scales)
         x_offs = (pick("offs_words", xw, l_offs, U32), offs_scales)
 
         nc.vector.tensor_copy(t5[2][:], tab_win[2][:].indirect(l5[:]))
@@ -135,10 +138,12 @@ def tile_picked_kqhopoverkinda_none_p_kernel(
         w2_q = [quantise("w2_%d" % h, deal(w2_bf[:, h, :], w2_raw, h), 2 * P) for h in range(2)]
         w1_raw = tile("w_raw", [P, PACK, N], F32)
         nc.sync.dma_start(w1_raw[:], w1.rearrange("(p j) c -> p j c", j=PACK))
-        for t in planes:
-            acc = product("bank_b%d" % t, w2_q[t // 2], t % 2, x_two)
-            nc.scalar.activation(bs_win[t][:, :N], acc[:], COPY, scale=b_scale[:, t : t + 1])
-            nc.scalar.activation(half_win[t][:, N:], acc[:], COPY, scale=c_scale[:, t : t + 1])
+        parts = [(0, "bank_a0", slice(0, N // 2)), (0, "bank_b0", slice(N // 2, N))]
+        parts += [(t, "bank_b%d" % t, slice(0, N)) for t in range(1, PACK)]
+        for t, bank, part in parts:
+            acc = product(bank, w2_q[t // 2], t % 2, x_two, part)
+            nc.scalar.activation(bs_win[t][:, part], acc[:], COPY, scale=b_scale[:, t : t + 1])
+            nc.scalar.activation(half_win[t][:, N:][:, part], acc[:], COPY, scale=c_scale[:, t : t + 1])
         for t in planes:
             nc.vector.tensor_tensor(u4[:, t, :], bs_win[t][:].indirect(l3[:]), half_win[t][:, N:], ALU.subtract)
 
@@ -186,5 +191,9 @@ def tile_picked_kqhopoverkinda_none_p_kernel(
                 nc.vector.tensor_tensor(prod[step][:], bs_win[step][:].indirect(l7[:]), t5[step][:], ALU.mult)
             if step > 0:
                 u = step - 1
-                nc.vector.tensor_tensor(res[u][:], tab_win[u][:].indirect(l6[:]), prod[u][:], ALU.add)
-                nc.sync.dma_start(out_rows[:, u, :], res[u][:])
+                pieces = 2 if u == PACK - 1 else 1
+                for i in range(pieces):
+                    cols = slice(i * N // pieces, (i + 1) * N // pieces)
+                    entries = l6[:, cols.start // 16 : cols.stop // 16]
+                    nc.vector.tensor_tensor(res[u][:, cols], tab_win[u][:].indirect(entries), prod[u][:, cols], ALU.add)
+                    nc.sync.dma_start(out_rows[:, u, cols], res[u][:, cols])

@@ -48,10 +48,8 @@ def tile_picked_kqhopoverkinda_none_p_kernel(
         st_win = [tile("st_win%d" % t, [P, 2 * N], F32) for t in planes]
 
         nc.gpsimd.memset(xs[:].bitcast(I32), 0)
-        for win in tab_win[:2] + bs_win[:2]:
+        for win in tab_win + bs_win[:1]:
             nc.vector.memset(win[:, N:], 0.0)
-        for win in tab_win[2:3] + bs_win[2:] + tab_win[3:]:
-            nc.gpsimd.memset(win[:, N:], 0.0)
 
         nc.sync.dma_start(tab_win[0][:, :N], tab_rows[:, 0, :])
         l5 = load_list("l5", n5)
@@ -63,22 +61,22 @@ def tile_picked_kqhopoverkinda_none_p_kernel(
         nc.sync.dma_start(w2_raw[:], w2.rearrange("(p j) c -> p j c", j=PACK))
         gb4 = tile("gb4", [P, PACK], F32)
         ga4 = tile("ga4", [P, PACK], F32)
-        nc.sync.dma_start(gb4[:], gb.rearrange("(p t) o -> p (t o)", t=PACK))
-        nc.sync.dma_start(ga4[:], ga.rearrange("(p t) o -> p (t o)", t=PACK))
         l_offs = load_list("l_offs", offs)
         nc.sync.dma_start(xw[:].bitcast(I32), x_words[0].rearrange("p n t -> p (n t)").bitcast(I32))
+        nc.sync.dma_start(gb4[:], gb.rearrange("(p t) o -> p (t o)", t=PACK))
         nc.sync.dma_start(tab_win[2][:, :N], tab_rows[:, 2, :])
         l3 = load_list("l3", n3)
         l4 = load_list("l4", n4)
+        nc.sync.dma_start(ga4[:], ga.rearrange("(p t) o -> p (t o)", t=PACK))
         l1 = load_list("l1", n1)
         l2 = load_list("l2", n2)
         l7 = load_list("l7", n7)
         l6 = load_list("l6", n6)
         nc.sync.dma_start(tab_win[3][:, :N], tab_rows[:, 3, :])
 
-        t5 = [tile("t5_%d" % u, [P, N], F32) for u in range(PACK - 1)]
+        t5 = [bs_win[u + 1][:, N:] for u in range(PACK - 1)]
         for u in range(2):
-            nc.vector.tensor_copy(t5[u][:], tab_win[u][:].indirect(l5[:]))
+            nc.vector.tensor_copy(t5[u], tab_win[u][:].indirect(l5[:]))
 
         sign2 = tile("sign2", [P, PACK], F32)
         sign = tile("sign", [P, PACK], F32)
@@ -132,7 +130,7 @@ def tile_picked_kqhopoverkinda_none_p_kernel(
         x_two = (pick("two_words", xw, l_two, U32, 2), two_scales)
         x_offs = (pick("offs_words", xw, l_offs, U32), offs_scales)
 
-        nc.vector.tensor_copy(t5[2][:], tab_win[2][:].indirect(l5[:]))
+        nc.vector.tensor_copy(t5[2], tab_win[2][:].indirect(l5[:]))
         u4 = tile("u4", [P, PACK, N], F32)
         w2_bf = tile("w2_bf", [P, 2, 2 * N], BF16)
         w2_q = [quantise("w2_%d" % h, deal(w2_bf[:, h, :], w2_raw, h), 2 * P) for h in range(2)]
@@ -177,18 +175,18 @@ def tile_picked_kqhopoverkinda_none_p_kernel(
         nc.vector.tensor_tensor(z2_bf[:], u_bf[:], v_bf[:], ALU.max)
         z2_q = quantise("z2", z2_bf[:], N)
         z_q = [quantise("z_0", z_dealt[0], 2 * P)]
-        t5.append(tile("z_dealt0", [P, N], F32))
-        nc.vector.tensor_copy(t5[3][:], tab_win[3][:].indirect(l5[:]))
+        t5.append(tile("z_dealt0", [P, N], F32)[:])
+        nc.vector.tensor_copy(t5[3], tab_win[3][:].indirect(l5[:]))
         z_q.append(quantise("z_1", z_dealt[1], 2 * P))
 
-        for u in planes:
-            acc = product("bank_b%d" % u, z_q[u // 2], u % 2, z2_q)
-            nc.scalar.activation(bs_win[u][:, :N], acc[:], COPY, scale=0.0625)
+        for u, bank, part in parts:
+            acc = product(bank, z_q[u // 2], u % 2, z2_q, part)
+            nc.scalar.activation(bs_win[u][:, part], acc[:], COPY, scale=0.0625)
         prod = [tile("prod%d" % u, [P, N], F32) for u in planes]
         res = [tile("res%d" % u, [P, N], F32) for u in planes]
         for step in range(PACK + 1):
             if step < PACK:
-                nc.vector.tensor_tensor(prod[step][:], bs_win[step][:].indirect(l7[:]), t5[step][:], ALU.mult)
+                nc.vector.tensor_tensor(prod[step][:], bs_win[step][:].indirect(l7[:]), t5[step], ALU.mult)
             if step > 0:
                 u = step - 1
                 pieces = 2 if u == PACK - 1 else 1

@@ -11,6 +11,7 @@ U8 = mybir.dt.uint8
 FP8X4 = mybir.dt.float8_e4m3fn_x4
 ALU = mybir.AluOpType
 ABS = mybir.ActivationFunctionType.Abs
+SIGN = mybir.ActivationFunctionType.Sign
 COPY = mybir.ActivationFunctionType.Copy
 
 P = 128
@@ -51,6 +52,9 @@ def tile_picked_kqhopoverkinda_none_p_kernel(
         for win in tab_win + bs_win[:1]:
             nc.vector.memset(win[:, N:], 0.0)
 
+        one_half = tile("one_half", [P, 1], F32)
+        nc.vector.memset(one_half[:], 0.5)
+
         nc.sync.dma_start(tab_win[0][:, :N], tab_rows[:, 0, :])
         l5 = load_list("l5", n5)
         nc.sync.dma_start(tab_win[1][:, :N], tab_rows[:, 1, :])
@@ -61,13 +65,13 @@ def tile_picked_kqhopoverkinda_none_p_kernel(
         nc.sync.dma_start(w2_raw[:], w2.rearrange("(p j) c -> p j c", j=PACK))
         gb4 = tile("gb4", [P, PACK], F32)
         ga4 = tile("ga4", [P, PACK], F32)
+        nc.sync.dma_start(gb4[:], gb.rearrange("(p t) o -> p (t o)", t=PACK))
+        nc.sync.dma_start(ga4[:], ga.rearrange("(p t) o -> p (t o)", t=PACK))
         l_offs = load_list("l_offs", offs)
         nc.sync.dma_start(xw[:].bitcast(I32), x_words[0].rearrange("p n t -> p (n t)").bitcast(I32))
-        nc.sync.dma_start(gb4[:], gb.rearrange("(p t) o -> p (t o)", t=PACK))
         nc.sync.dma_start(tab_win[2][:, :N], tab_rows[:, 2, :])
         l3 = load_list("l3", n3)
         l4 = load_list("l4", n4)
-        nc.sync.dma_start(ga4[:], ga.rearrange("(p t) o -> p (t o)", t=PACK))
         l1 = load_list("l1", n1)
         l2 = load_list("l2", n2)
         l7 = load_list("l7", n7)
@@ -84,12 +88,13 @@ def tile_picked_kqhopoverkinda_none_p_kernel(
         c_scale = tile("c_scale", [P, PACK], F32)
         a_scale = tile("a_scale", [P, PACK], F32)
         h_scale = tile("h_scale", [P, PACK], F32)
-        nc.gpsimd.tensor_scalar(sign2[:], gb4[:], 0.0, 2.0, ALU.is_ge, ALU.mult)
-        nc.gpsimd.tensor_scalar(sign[:], sign2[:], -1.0, None, ALU.add)
+        nc.scalar.activation(sign2[:], gb4[:], SIGN)
+        nc.scalar.activation(sign[:], sign2[:], SIGN, bias=one_half[:])
         nc.scalar.activation(b_scale[:], gb4[:], ABS)
-        nc.gpsimd.tensor_tensor(a_scale[:], ga4[:], sign[:], ALU.mult)
+        for t in planes:
+            nc.scalar.activation(a_scale[:, t : t + 1], ga4[:, t : t + 1], COPY, scale=sign[:, t : t + 1])
         nc.scalar.activation(c_scale[:], gb4[:], ABS, scale=0.75)
-        nc.gpsimd.tensor_scalar(h_scale[:], a_scale[:], -0.5, None, ALU.mult)
+        nc.scalar.activation(h_scale[:], a_scale[:], COPY, scale=-0.5)
 
         def pick(name, table, lst, dtype, pieces=1):
             picked = tile(name, [P, N], dtype)

from contextlib import ExitStack

import concourse.mybir as mybir

F32 = mybir.dt.float32
BF16 = mybir.dt.bfloat16
I32 = mybir.dt.int32
U32 = mybir.dt.uint32
U16 = mybir.dt.uint16
U8 = mybir.dt.uint8
FP8X4 = mybir.dt.float8_e4m3fn_x4
ALU = mybir.AluOpType
ABS = mybir.ActivationFunctionType.Abs
SIGN = mybir.ActivationFunctionType.Sign
COPY = mybir.ActivationFunctionType.Copy

P = 128
PACK = 4
N = 512
T = 2048
FLOPS = 3 * 2 * 512 * 512 * 512


def tile_picked_kqhopoverkinda_none_p_kernel(
    tc, x_words, x_scales, w1, w2, ga, gb, tab, offs, two, n1, n2, n3, n4, n5, n6, n7, out
):
    nc = tc.nc
    with ExitStack() as ctx:
        sb = ctx.enter_context(tc.tile_pool(name="sb", bufs=1))
        ps = ctx.enter_context(tc.psum_pool(name="ps", bufs=1))

        def tile(name, shape, dtype):
            return sb.tile(shape, dtype, name=name, align_bytes=64)

        def load_list(name, src):
            lst = tile(name, [P, N // 16], U16)
            nc.sync.dma_start(lst[:], src)
            return lst

        planes = range(PACK)
        tab_rows = tab.rearrange("(p u) j -> p u j", u=PACK)
        out_rows = out.rearrange("(p u) v -> p u v", u=PACK)

        xw = tile("xw", [P, T], U32)
        xs = tile("xs", [P, T], U8)
        tab_win = [tile("tab_win%d" % u, [P, 2 * N], F32) for u in planes]
        bs_win = [tile("bs_win%d" % t, [P, 2 * N], F32) for t in planes]
        half_win = [tile("half_win%d" % t, [P, 2 * N], F32) for t in planes]
        st_win = [tile("st_win%d" % t, [P, 2 * N], F32) for t in planes]

        nc.gpsimd.memset(xs[:].bitcast(I32), 0)
        for win in tab_win + bs_win[:1]:
            nc.vector.memset(win[:, N:], 0.0)

        one_half = tile("one_half", [P, 1], F32)
        nc.vector.memset(one_half[:], 0.5)

        nc.sync.dma_start(tab_win[0][:, :N], tab_rows[:, 0, :])
        l5 = load_list("l5", n5)
        nc.sync.dma_start(tab_win[1][:, :N], tab_rows[:, 1, :])
        l_two = load_list("l_two", two)
        for q in range(4):
            nc.scalar.dma_start(xs[32 * q : 32 * q + 4, :].bitcast(I32), x_scales[0, 4 * q : 4 * q + 4, :].bitcast(I32))
        w2_raw = tile("w_raw", [P, PACK, N], F32)
        nc.sync.dma_start(w2_raw[:], w2.rearrange("(p j) c -> p j c", j=PACK))
        gb4 = tile("gb4", [P, PACK], F32)
        ga4 = tile("ga4", [P, PACK], F32)
        nc.sync.dma_start(gb4[:], gb.rearrange("(p t) o -> p (t o)", t=PACK))
        nc.sync.dma_start(ga4[:], ga.rearrange("(p t) o -> p (t o)", t=PACK))
        l_offs = load_list("l_offs", offs)
        nc.sync.dma_start(xw[:].bitcast(I32), x_words[0].rearrange("p n t -> p (n t)").bitcast(I32))
        nc.sync.dma_start(tab_win[2][:, :N], tab_rows[:, 2, :])
        l3 = load_list("l3", n3)
        l4 = load_list("l4", n4)
        l1 = load_list("l1", n1)
        l2 = load_list("l2", n2)
        l7 = load_list("l7", n7)
        l6 = load_list("l6", n6)
        nc.sync.dma_start(tab_win[3][:, :N], tab_rows[:, 3, :])

        t5 = [bs_win[u + 1][:, N:] for u in range(PACK - 1)]
        for u in range(2):
            nc.vector.tensor_copy(t5[u], tab_win[u][:].indirect(l5[:]))

        sign2 = tile("sign2", [P, PACK], F32)
        sign = tile("sign", [P, PACK], F32)
        b_scale = tile("b_scale", [P, PACK], F32)
        c_scale = tile("c_scale", [P, PACK], F32)
        a_scale = tile("a_scale", [P, PACK], F32)
        h_scale = tile("h_scale", [P, PACK], F32)
        nc.scalar.activation(sign2[:], gb4[:], SIGN)
        nc.scalar.activation(sign[:], sign2[:], SIGN, bias=one_half[:])
        nc.scalar.activation(b_scale[:], gb4[:], ABS)
        for t in planes:
            nc.scalar.activation(a_scale[:, t : t + 1], ga4[:, t : t + 1], COPY, scale=sign[:, t : t + 1])
        nc.scalar.activation(c_scale[:], gb4[:], ABS, scale=0.75)
        nc.scalar.activation(h_scale[:], a_scale[:], COPY, scale=-0.5)

        def pick(name, table, lst, dtype, pieces=1):
            picked = tile(name, [P, N], dtype)
            for i in range(pieces):
                cols = slice(i * N // pieces, (i + 1) * N // pieces)
                nc.vector.tensor_copy(picked[:, cols], table[:].indirect(lst[:, cols.start // 16 : cols.stop // 16]))
            return picked

        def deal(dealt, raw, h):
            nc.scalar.copy(
                dealt.rearrange("p (e m j) -> p m j e", e=2, j=PACK),
                raw[:].rearrange("p j (m t) -> p m j t", t=PACK)[:, :, :, 2 * h : 2 * h + 2],
            )
            return dealt

        def quantise(name, src, width):
            codes = tile(name + "_codes", [P, width], U32)
            scales = tile(name + "_scales", [P, width], U8)
            nc.vector.quantize_mx(out=codes[:].bitcast(FP8X4), scales=scales[:], in_=src)
            return codes, scales

        def product(bank, stationary, e, moving, part=slice(0, N)):
            acc = ps.tile([P, part.stop - part.start], F32, name=bank)
            cols = slice(e * P, (e + 1) * P)
            nc.tensor.matmul_mx(
                out=acc[:],
                lhsT=stationary[0][:, cols].bitcast(FP8X4),
                lhsT_scale=stationary[1][:, cols],
                rhs=moving[0][:, part].bitcast(FP8X4),
                rhs_scale=moving[1][:, part],
                start=True,
                stop=True,
            )
            return acc

        two_scales = pick("two_scales", xs, l_two, U8)
        offs_scales = pick("offs_scales", xs, l_offs, U8)
        x_two = (pick("two_words", xw, l_two, U32, 2), two_scales)
        x_offs = (pick("offs_words", xw, l_offs, U32), offs_scales)

        nc.vector.tensor_copy(t5[2], tab_win[2][:].indirect(l5[:]))
        u4 = tile("u4", [P, PACK, N], F32)
        w2_bf = tile("w2_bf", [P, 2, 2 * N], BF16)
        w2_q = [quantise("w2_%d" % h, deal(w2_bf[:, h, :], w2_raw, h), 2 * P) for h in range(2)]
        w1_raw = tile("w_raw", [P, PACK, N], F32)
        nc.sync.dma_start(w1_raw[:], w1.rearrange("(p j) c -> p j c", j=PACK))
        parts = [(0, "bank_a0", slice(0, N // 2)), (0, "bank_b0", slice(N // 2, N))]
        parts += [(t, "bank_b%d" % t, slice(0, N)) for t in range(1, PACK)]
        for t, bank, part in parts:
            acc = product(bank, w2_q[t // 2], t % 2, x_two, part)
            nc.scalar.activation(bs_win[t][:, part], acc[:], COPY, scale=b_scale[:, t : t + 1])
            nc.scalar.activation(half_win[t][:, N:][:, part], acc[:], COPY, scale=c_scale[:, t : t + 1])
        for t in planes:
            nc.vector.tensor_tensor(u4[:, t, :], bs_win[t][:].indirect(l3[:]), half_win[t][:, N:], ALU.subtract)

        w1_bf = tile("v4", [P, 2, 2 * N], BF16)
        w1_q = [quantise("w1_%d" % h, deal(w1_bf[:, h, :], w1_raw, h), 2 * P) for h in range(2)]
        v4 = tile("v4", [P, PACK, N], F32)
        for t in planes:
            nc.vector.tensor_tensor(v4[:, t, :], bs_win[t][:].indirect(l4[:]), half_win[t][:, N:], ALU.subtract)
        for t in planes:
            acc = product("bank_a%d" % t, w1_q[t // 2], t % 2, x_offs)
            nc.scalar.activation(half_win[t][:, :N], acc[:], COPY, scale=h_scale[:, t : t + 1])
            nc.scalar.activation(st_win[t][:, N:], acc[:], COPY, scale=a_scale[:, t : t + 1])
        st4 = tile("st4", [P, PACK, N], F32)
        u_bf = tile("offs_words", [P, N * PACK], BF16)
        v_bf = tile("offs_scales", [P, N * PACK], BF16)
        for t in planes:
            src, dst, h = (u4, v4)[t // 2], (u_bf, v_bf)[t // 2], t % 2
            nc.scalar.copy(
                dst[:, h * 2 * N : (h + 1) * 2 * N].rearrange("p (c i t) -> p c t i", i=4, t=PACK),
                src[:, :, h * N // 2 : (h + 1) * N // 2].rearrange("p t (c i) -> p c t i", i=4),
            )
            nc.vector.tensor_tensor(st_win[t][:, :N], half_win[t][:].indirect(l1[:]), st_win[t][:, N:], ALU.subtract)
            nc.scalar.activation(st4[:, t, :], st_win[t][:, :N], COPY, scale=-1.0)

        z4 = tile("z4", [P, PACK, N], F32)
        for t in planes:
            nc.vector.tensor_tensor(z4[:, t, :], st_win[t][:].indirect(l2[:]), st4[:, t, :], ALU.add)

        z_dealt = [deal(tile("z_dealt%d" % h, [P, 2 * N], BF16)[:], z4, h) for h in range(2)]
        z2_bf = tile("st4", [P, N * PACK], BF16)
        nc.vector.tensor_tensor(z2_bf[:], u_bf[:], v_bf[:], ALU.max)
        z2_q = quantise("z2", z2_bf[:], N)
        z_q = [quantise("z_0", z_dealt[0], 2 * P)]
        t5.append(tile("z_dealt0", [P, N], F32)[:])
        nc.vector.tensor_copy(t5[3], tab_win[3][:].indirect(l5[:]))
        z_q.append(quantise("z_1", z_dealt[1], 2 * P))

        for u, bank, part in parts:
            acc = product(bank, z_q[u // 2], u % 2, z2_q, part)
            nc.scalar.activation(bs_win[u][:, part], acc[:], COPY, scale=0.0625)
        prod = [tile("prod%d" % u, [P, N], F32) for u in planes]
        res = [tile("res%d" % u, [P, N], F32) for u in planes]
        for step in range(PACK + 1):
            if step < PACK:
                nc.vector.tensor_tensor(prod[step][:], bs_win[step][:].indirect(l7[:]), t5[step], ALU.mult)
            if step > 0:
                u = step - 1
                pieces = 2 if u == PACK - 1 else 1
                for i in range(pieces):
                    cols = slice(i * N // pieces, (i + 1) * N // pieces)
                    entries = l6[:, cols.start // 16 : cols.stop // 16]
                    nc.vector.tensor_tensor(res[u][:, cols], tab_win[u][:].indirect(entries), prod[u][:, cols], ALU.add)
                    nc.sync.dma_start(out_rows[:, u, cols], res[u][:, cols])
